import numpy as np
import ml_dtypes


def mxq(x, axis, fmt="e4m3"):
    dtype, down = {"e4m3": (ml_dtypes.float8_e4m3fn, 7), "e5m2": (ml_dtypes.float8_e5m2, 14)}[fmt]
    v = np.moveaxis(np.asarray(x, np.float32).astype(ml_dtypes.bfloat16).astype(np.float64), axis, -1)
    blocks = v.reshape(v.shape[:-1] + (-1, 32))
    amax = np.abs(blocks).max(-1, keepdims=True)
    byte = np.maximum(np.where(amax > 0, np.frexp(amax)[1] - 1 + 127, 0) - down, 1)
    scale = np.exp2(byte - 127.0)
    codes = (blocks / scale).astype(np.float32).astype(dtype).astype(np.float64)
    return np.moveaxis((codes * scale).reshape(v.shape), -1, axis)


WIDE = False


def mx_kscale(k):
    if not WIDE:
        return np.ones(k)
    levels = np.array([30, -30])
    if k % 512:
        return np.exp2(np.random.permutation(np.resize(levels, k // 32))).repeat(32)
    a = np.empty((k // 512, 16))
    for p in range(k // 512):
        a[p, :8] = np.random.permutation(np.resize(levels, 8))
        for g in range(8):
            far = levels[np.abs(levels - a[p, g]) >= 10]
            a[p, g + 8] = far[np.random.randint(len(far))]
    return np.exp2(a.ravel()).repeat(32)


def f64(x):
    return np.asarray(x).astype(np.float64)


def striped(idx):
    return np.tile(np.asarray(idx).reshape(-1, 16).T, (8, 1)).astype(np.uint16)


def unstriped(offs):
    return offs[:16].T.reshape(-1).astype(np.int64)


E2M1 = np.array([0.0, 0.5, 1.0, 1.5, 2.0, 3.0, 4.0, 6.0, -0.0, -0.5, -1.0, -1.5, -2.0, -3.0, -4.0, -6.0])


def pack_weight(w, fmt):
    k, n = w.shape
    w = f64(np.asarray(w, np.float32).astype(ml_dtypes.bfloat16)).reshape(k // 32, 32, n)
    amax = np.abs(w).max(1)
    if fmt == "e4m3":
        byte = np.frexp(amax)[1] - 1 + 127 - 7
    else:
        mant, ex = np.frexp(amax / 6.0)
        byte = np.where(mant > 0.5, ex, ex - 1) + 127
    byte = np.clip(np.where(amax > 0, byte, 1), 1, 254)
    scaled = (w * np.exp2(127.0 - byte)[:, None, :]).reshape(k, n).astype(np.float32)
    by_word = np.ascontiguousarray(scaled.reshape(k // 512, 128, 4, n).transpose(0, 1, 3, 2))
    if fmt == "e4m3":
        words = by_word.astype(ml_dtypes.float8_e4m3fn).view(np.uint8)
    else:
        c = by_word.astype(ml_dtypes.float4_e2m1fn).view(np.uint8) & 0xF
        words = (c[..., 0::2] | (c[..., 1::2] << 4)).reshape(k // 512, 128, 2 * n)
    return np.ascontiguousarray(words), np.ascontiguousarray(byte.astype(np.uint8).reshape(k // 512, 16, n))


def unpack_weight(words, scales, fmt):
    g, _, n = scales.shape
    words = np.ascontiguousarray(words).reshape(g, 128, n, -1)
    if fmt == "e4m3":
        vals = words.view(ml_dtypes.float8_e4m3fn).astype(np.float64)
    else:
        nib = np.empty((g, 128, n, 4), np.uint8)
        nib[..., 0::2] = words & 0xF
        nib[..., 1::2] = words >> 4
        vals = E2M1[nib]
    vals = vals * np.repeat(np.exp2(scales.astype(np.float64) - 127.0), 8, axis=1)[..., None]
    return vals.transpose(0, 1, 3, 2).reshape(g * 512, n)


K, T, J, R, C, O, N = 512, 2048, 256, 512, 512, 256, 256


def setup_inputs():
    n = np.random.standard_normal
    idx = np.random.permutation(T)[:J]
    idx2 = np.random.permutation(T)[:J]
    idx3 = np.random.permutation(C)[:J]
    idx4 = np.random.permutation(C)[:J]
    idx5 = np.random.permutation(C)[:O]
    idx6 = np.random.permutation(C)[:O]
    fk = mx_kscale(K)
    fr = mx_kscale(R)
    xtp = pack_weight(n((K, T)) / fk[:, None], "e2m1")
    wp = pack_weight(n((K, R)) * 1 / np.sqrt(K) * fk[:, None] * fr, "e4m3")
    wbp = pack_weight(n((R, N)) * 1 / np.sqrt(R) / fr[:, None], "e2m1")
    return {
        "xt_words": xtp[0],
        "xt_scales": xtp[1],
        "w_words": wp[0],
        "w_scales": wp[1],
        "wb_words": wbp[0],
        "wb_scales": wbp[1],
        "offs": striped(idx),
        "offs2": striped(idx2),
        "offs3": striped(idx3),
        "offs4": striped(idx4),
        "offs5": striped(idx5),
        "offs6": striped(idx6),
    }


def reference(xt_words, xt_scales, w_words, w_scales, wb_words, wb_scales, offs, offs2, offs3, offs4, offs5, offs6):
    idx = unstriped(offs)
    idx2 = unstriped(offs2)
    idx3 = unstriped(offs3)
    idx4 = unstriped(offs4)
    idx5 = unstriped(offs5)
    idx6 = unstriped(offs6)
    xtu = unpack_weight(xt_words, xt_scales, "e2m1")
    wu = unpack_weight(w_words, w_scales, "e4m3")
    wbu = unpack_weight(wb_words, wb_scales, "e2m1")
    xtidxg = xtu[:, idx]
    a = wu.T @ xtidxg
    xtidx2g = xtu[:, idx2]
    b = wu.T @ xtidx2g
    pw = np.zeros((R, C))
    pw[:, idx3] = a
    pv = np.zeros((R, C))
    pv[:, idx4] = b
    hid = np.abs(pw[:, idx5] - pv[:, idx6])
    hidq = mxq(hid, 0, "e5m2")
    y = wbu.T @ hidq
    return y

@@ -1,0 +1,174 @@
+from contextlib import ExitStack
+
+import concourse.mybir as mybir
+
+K, T, J, R, C, O, N = 512, 2048, 256, 512, 512, 256, 256
+FLOPS = 2 * K * R * 2 * J + 2 * R * N * O
+
+F32 = mybir.dt.float32
+BF16 = mybir.dt.bfloat16
+I32 = mybir.dt.int32
+U32 = mybir.dt.uint32
+U16 = mybir.dt.uint16
+U8 = mybir.dt.uint8
+E4M3X4 = mybir.dt.float8_e4m3fn_x4
+E5M2X4 = mybir.dt.float8_e5m2_x4
+E2M1X4 = mybir.dt.float4_e2m1fn_x4
+ACT = mybir.ActivationFunctionType
+ALU = mybir.AluOpType
+
+P = 128
+PACK = 4
+HALF = O // 2
+
+
+def load_scale_rows(queue, plane, scales, q):
+    queue.dma_start(out=plane[32 * q : 32 * q + 4, :].bitcast(I32), in_=scales[0, 4 * q : 4 * q + 4, :].bitcast(I32))
+
+
+def tile_list_tied_twoboards_one_plain_kernel(
+    tc, xt_words, xt_scales, w_words, w_scales, wb_words, wb_scales, offs, offs2, offs3, offs4, offs5, offs6, out
+):
+    nc = tc.nc
+    with ExitStack() as ctx:
+        lists = ctx.enter_context(tc.tile_pool(name="lists", bufs=1))
+        keep = ctx.enter_context(tc.tile_pool(name="keep", bufs=1))
+        psum = ctx.enter_context(tc.psum_pool(name="psum", bufs=8))
+
+        l_tok_a = lists.tile([P, J // 16], U16, name="l_tok_a")
+        l_tok_b = lists.tile([P, J // 16], U16, name="l_tok_b")
+        l_put_a = lists.tile([P, J // 16], U16, name="l_put_a")
+        l_put_b = lists.tile([P, J // 16], U16, name="l_put_b")
+        l_get_a = lists.tile([P, O // 16], U16, name="l_get_a")
+        l_get_b = lists.tile([P, O // 16], U16, name="l_get_b")
+
+        x_words = keep.tile([P, T], U16, name="x_words", align_bytes=64)
+        x_plane = keep.tile([P, T], U8, name="x_plane", align_bytes=64)
+        w_raw = keep.tile([P, R], U32, name="w_raw", align_bytes=64)
+        w_raw_plane = keep.tile([P, R], U8, name="w_raw_plane", align_bytes=64)
+        w_codes = keep.tile([P, R], U32, name="w_codes", align_bytes=64)
+        w_plane = keep.tile([P, R], U8, name="w_plane", align_bytes=64)
+        wb_codes = keep.tile([P, 2 * N], U8, name="wb_codes", align_bytes=64)
+        wb_plane = keep.tile([P, N], U8, name="wb_plane", align_bytes=64)
+
+        nc.vector.memset(x_plane[:].bitcast(I32), 0)
+        nc.vector.memset(w_raw_plane[:].bitcast(I32), 0)
+
+        nc.sync.dma_start(l_tok_a[:], offs)
+        nc.sync.dma_start(l_tok_b[:], offs2)
+        nc.sync.dma_start(out=x_words[:].bitcast(I32), in_=xt_words[0].bitcast(I32))
+        nc.gpsimd.dma_start(out=w_raw[:].bitcast(I32), in_=w_words[0].rearrange("p n t -> p (n t)").bitcast(I32))
+        for q in range(4):
+            load_scale_rows(nc.scalar, x_plane, xt_scales, q)
+        for q in range(3):
+            load_scale_rows(nc.sync, w_raw_plane, w_scales, q)
+        load_scale_rows(nc.gpsimd, w_raw_plane, w_scales, 3)
+        nc.sync.dma_start(l_put_a[:], offs3)
+        nc.sync.dma_start(l_put_b[:], offs4)
+        nc.sync.dma_start(l_get_a[:], offs5)
+        nc.sync.dma_start(l_get_b[:], offs6)
+
+        board_a = [keep.tile([P, C], F32, name="board_a%d" % t) for t in range(PACK)]
+        board_b = [keep.tile([P, C], F32, name="board_b%d" % t) for t in range(PACK)]
+        for t in range(PACK):
+            nc.gpsimd.memset(board_a[t][:], 0.0)
+            nc.gpsimd.memset(board_b[t][:], 0.0)
+        nc.gpsimd.memset(wb_plane[:].bitcast(I32), 0)
+        nc.gpsimd.dma_start(out=wb_codes[:].bitcast(I32), in_=wb_words[0].bitcast(I32))
+        for q in range(4):
+            load_scale_rows(nc.gpsimd, wb_plane, wb_scales, q)
+
+        nc.scalar.copy(
+            out=w_codes[:].rearrange("p (t m) -> p m t", t=PACK), in_=w_raw[:].rearrange("p (m t) -> p m t", t=PACK)
+        )
+
+        xa_words = keep.tile([P, J], U16, name="xa_words", align_bytes=64)
+        xb_words = keep.tile([P, J], U16, name="xb_words", align_bytes=64)
+        xa_plane = keep.tile([P, J], U8, name="xa_plane", align_bytes=64)
+        xb_plane = keep.tile([P, J], U8, name="xb_plane", align_bytes=64)
+        nc.vector.tensor_copy(xa_plane[:], x_plane[:].indirect(l_tok_a[:]))
+        nc.vector.tensor_copy(xb_plane[:], x_plane[:].indirect(l_tok_b[:]))
+        nc.vector.tensor_copy(
+            out=w_plane[:].rearrange("p (t m) -> p t m", t=PACK),
+            in_=w_raw_plane[:].rearrange("p (m t) -> p t m", t=PACK),
+        )
+        nc.vector.tensor_copy(xa_words[:], x_words[:].indirect(l_tok_a[:]))
+        nc.vector.tensor_copy(xb_words[:], x_words[:].indirect(l_tok_b[:]))
+
+        def first_product(t, words, plane):
+            acc = psum.tile([P, J], F32, name="acc")
+            cols = slice(P * t, P * (t + 1))
+            nc.tensor.matmul_mx(
+                out=acc[:],
+                lhsT=w_codes[:, cols].bitcast(E4M3X4),
+                lhsT_scale=w_plane[:, cols],
+                rhs=words[:].bitcast(E2M1X4),
+                rhs_scale=plane[:],
+                start=True,
+                stop=True,
+            )
+            return acc
+
+        acc_a, acc_b = [], []
+        for t0 in range(0, PACK, 2):
+            acc_a.extend(first_product(t, xa_words, xa_plane) for t in (t0, t0 + 1))
+            acc_b.extend(first_product(t, xb_words, xb_plane) for t in (t0, t0 + 1))
+
+        a_vals = [keep.tile([P, J], F32, name="a_vals%d" % t) for t in range(PACK)]
+        b_vals = [keep.tile([P, J], F32, name="b_vals%d" % t) for t in range(PACK)]
+        a_read = [keep.tile([P, O], F32, name="a_read%d" % t) for t in range(PACK)]
+        diff = keep.tile([P, PACK, O], F32, name="diff")
+
+        def leave_psum(t):
+            nc.scalar.copy(out=a_vals[t][:], in_=acc_a[t][:])
+            nc.vector.tensor_copy(out=b_vals[t][:], in_=acc_b[t][:])
+
+        def put(t):
+            nc.scalar.activation(board_a[t][:].indirect(l_put_a[:]), a_vals[t][:], ACT.Copy)
+            nc.vector.tensor_copy(board_b[t][:].indirect(l_put_b[:]), b_vals[t][:])
+
+        def get(t):
+            nc.scalar.activation(a_read[t][:], board_a[t][:].indirect(l_get_a[:]), ACT.Copy)
+            nc.vector.tensor_tensor(diff[:, t, :], board_b[t][:].indirect(l_get_b[:]), a_read[t][:], ALU.subtract)
+
+        leave_psum(0)
+        for t in range(PACK):
+            put(t)
+            if t + 1 < PACK:
+                leave_psum(t + 1)
+            get(t)
+
+        hid = [keep.tile([P, HALF, PACK], BF16, name="hid%d" % h, align_bytes=64) for h in range(2)]
+        hid_codes = keep.tile([P, O], U32, name="hid_codes", align_bytes=64)
+        hid_plane = keep.tile([P, O], U8, name="hid_plane", align_bytes=64)
+        by_column = diff[:].rearrange("p t o -> p o t")
+        nc.scalar.activation(hid[0][:], by_column[:, 0:HALF, :], ACT.Abs)
+        nc.vector.scalar_tensor_tensor(
+            hid[1][:], by_column[:, HALF:O, :], -1.0, by_column[:, HALF:O, :], ALU.mult, ALU.max
+        )
+        for h in range(2):
+            cols = slice(HALF * h, HALF * (h + 1))
+            nc.vector.quantize_mx(
+                out=hid_codes[:, cols].bitcast(E5M2X4),
+                scales=hid_plane[:, cols],
+                in_=hid[h][:].rearrange("p o t -> p (o t)"),
+            )
+
+        result = [keep.tile([P, O], F32, name="result%d" % n) for n in range(N // P)]
+        for n in range(N // P):
+            acc = psum.tile([P, O], F32, name="acc")
+            nc.tensor.matmul_mx(
+                out=acc[:],
+                lhsT=wb_codes[:, 2 * P * n : 2 * P * (n + 1)].bitcast(E2M1X4),
+                lhsT_scale=wb_plane[:, P * n : P * (n + 1)],
+                rhs=hid_codes[:].bitcast(E5M2X4),
+                rhs_scale=hid_plane[:],
+                start=True,
+                stop=True,
+            )
+            if n == 0:
+                nc.scalar.copy(out=result[n][:], in_=acc[:])
+                nc.scalar.dma_start(out=out[P * n : P * (n + 1), :], in_=result[n][:])
+            else:
+                nc.vector.tensor_copy(out=result[n][:], in_=acc[:])
+                nc.sync.dma_start(out=out[P * n : P * (n + 1), :], in_=result[n][:])

@@ -42,8 +42,8 @@ def tile_list_tied_twoboards_one_plain_kernel(
         l_get_a = lists.tile([P, O // 16], U16, name="l_get_a")
         l_get_b = lists.tile([P, O // 16], U16, name="l_get_b")
 
-        x_words = keep.tile([P, T], U16, name="x_words", align_bytes=64)
-        x_plane = keep.tile([P, T], U8, name="x_plane", align_bytes=64)
+        x_words = keep.tile([P, T], U16, name="x_words", tag="x_words", align_bytes=64)
+        x_plane = keep.tile([P, T], U8, name="x_plane", tag="x_plane", align_bytes=64)
         w_raw = keep.tile([P, R], U32, name="w_raw", align_bytes=64)
         w_raw_plane = keep.tile([P, R], U8, name="w_raw_plane", align_bytes=64)
         w_codes = keep.tile([P, R], U32, name="w_codes", align_bytes=64)
@@ -53,30 +53,29 @@ def tile_list_tied_twoboards_one_plain_kernel(
 
         nc.vector.memset(x_plane[:].bitcast(I32), 0)
         nc.vector.memset(w_raw_plane[:].bitcast(I32), 0)
+        nc.vector.memset(wb_plane[:].bitcast(I32), 0)
 
         nc.sync.dma_start(l_tok_a[:], offs)
         nc.sync.dma_start(l_tok_b[:], offs2)
         nc.sync.dma_start(out=x_words[:].bitcast(I32), in_=xt_words[0].bitcast(I32))
-        nc.gpsimd.dma_start(out=w_raw[:].bitcast(I32), in_=w_words[0].rearrange("p n t -> p (n t)").bitcast(I32))
+        nc.sync.dma_start(out=w_raw[:].bitcast(I32), in_=w_words[0].rearrange("p n t -> p (n t)").bitcast(I32))
         for q in range(4):
             load_scale_rows(nc.scalar, x_plane, xt_scales, q)
-        for q in range(3):
+        for q in range(4):
             load_scale_rows(nc.sync, w_raw_plane, w_scales, q)
-        load_scale_rows(nc.gpsimd, w_raw_plane, w_scales, 3)
         nc.sync.dma_start(l_put_a[:], offs3)
         nc.sync.dma_start(l_put_b[:], offs4)
         nc.sync.dma_start(l_get_a[:], offs5)
         nc.sync.dma_start(l_get_b[:], offs6)
-
-        board_a = [keep.tile([P, C], F32, name="board_a%d" % t) for t in range(PACK)]
-        board_b = [keep.tile([P, C], F32, name="board_b%d" % t) for t in range(PACK)]
-        for t in range(PACK):
-            nc.gpsimd.memset(board_a[t][:], 0.0)
-            nc.gpsimd.memset(board_b[t][:], 0.0)
-        nc.gpsimd.memset(wb_plane[:].bitcast(I32), 0)
-        nc.gpsimd.dma_start(out=wb_codes[:].bitcast(I32), in_=wb_words[0].bitcast(I32))
+        nc.sync.dma_start(out=wb_codes[:].bitcast(I32), in_=wb_words[0].bitcast(I32))
         for q in range(4):
-            load_scale_rows(nc.gpsimd, wb_plane, wb_scales, q)
+            load_scale_rows(nc.sync, wb_plane, wb_scales, q)
+
+        board_a = [keep.tile([P, C], F32, name="board_a%d" % t) for t in range(PACK - 1)]
+        board_b = [keep.tile([P, C], F32, name="board_b%d" % t) for t in range(PACK - 1)]
+        for t in range(PACK - 1):
+            nc.vector.memset(board_a[t][:], 0.0)
+            nc.vector.memset(board_b[t][:], 0.0)
 
         nc.scalar.copy(
             out=w_codes[:].rearrange("p (t m) -> p m t", t=PACK), in_=w_raw[:].rearrange("p (m t) -> p m t", t=PACK)
@@ -88,12 +87,16 @@ def tile_list_tied_twoboards_one_plain_kernel(
         xb_plane = keep.tile([P, J], U8, name="xb_plane", align_bytes=64)
         nc.vector.tensor_copy(xa_plane[:], x_plane[:].indirect(l_tok_a[:]))
         nc.vector.tensor_copy(xb_plane[:], x_plane[:].indirect(l_tok_b[:]))
+        nc.vector.tensor_copy(xa_words[:], x_words[:].indirect(l_tok_a[:]))
+        nc.vector.tensor_copy(xb_words[:], x_words[:].indirect(l_tok_b[:]))
         nc.vector.tensor_copy(
             out=w_plane[:].rearrange("p (t m) -> p t m", t=PACK),
             in_=w_raw_plane[:].rearrange("p (m t) -> p t m", t=PACK),
         )
-        nc.vector.tensor_copy(xa_words[:], x_words[:].indirect(l_tok_a[:]))
-        nc.vector.tensor_copy(xb_words[:], x_words[:].indirect(l_tok_b[:]))
+        board_a.append(keep.tile([P, C], F32, name="board_a3", tag="x_plane", align_bytes=64))
+        board_b.append(keep.tile([P, C], F32, name="board_b3", tag="x_words", align_bytes=64))
+        nc.vector.memset(board_a[PACK - 1][:], 0.0)
+        nc.vector.memset(board_b[PACK - 1][:], 0.0)
 
         def first_product(t, words, plane):
             acc = psum.tile([P, J], F32, name="acc")
@@ -110,14 +113,14 @@ def tile_list_tied_twoboards_one_plain_kernel(
             return acc
 
         acc_a, acc_b = [], []
-        for t0 in range(0, PACK, 2):
-            acc_a.extend(first_product(t, xa_words, xa_plane) for t in (t0, t0 + 1))
-            acc_b.extend(first_product(t, xb_words, xb_plane) for t in (t0, t0 + 1))
+        for t in range(PACK):
+            acc_a.append(first_product(t, xa_words, xa_plane))
+            acc_b.append(first_product(t, xb_words, xb_plane))
 
         a_vals = [keep.tile([P, J], F32, name="a_vals%d" % t) for t in range(PACK)]
         b_vals = [keep.tile([P, J], F32, name="b_vals%d" % t) for t in range(PACK)]
         a_read = [keep.tile([P, O], F32, name="a_read%d" % t) for t in range(PACK)]
-        diff = keep.tile([P, PACK, O], F32, name="diff")
+        diff = [keep.tile([P, PACK, HALF], F32, name="diff%d" % h) for h in range(2)]
 
         def leave_psum(t):
             nc.scalar.copy(out=a_vals[t][:], in_=acc_a[t][:])
@@ -129,7 +132,11 @@ def tile_list_tied_twoboards_one_plain_kernel(
 
         def get(t):
             nc.scalar.activation(a_read[t][:], board_a[t][:].indirect(l_get_a[:]), ACT.Copy)
-            nc.vector.tensor_tensor(diff[:, t, :], board_b[t][:].indirect(l_get_b[:]), a_read[t][:], ALU.subtract)
+            for h in range(2):
+                picks = l_get_b[:, HALF // 16 * h : HALF // 16 * (h + 1)]
+                nc.vector.tensor_tensor(
+                    diff[h][:, t, :], board_b[t][:].indirect(picks), a_read[t][:, HALF * h : HALF * (h + 1)], ALU.subtract
+                )
 
         leave_psum(0)
         for t in range(PACK):
@@ -139,36 +146,37 @@ def tile_list_tied_twoboards_one_plain_kernel(
             get(t)
 
         hid = [keep.tile([P, HALF, PACK], BF16, name="hid%d" % h, align_bytes=64) for h in range(2)]
-        hid_codes = keep.tile([P, O], U32, name="hid_codes", align_bytes=64)
-        hid_plane = keep.tile([P, O], U8, name="hid_plane", align_bytes=64)
-        by_column = diff[:].rearrange("p t o -> p o t")
-        nc.scalar.activation(hid[0][:], by_column[:, 0:HALF, :], ACT.Abs)
-        nc.vector.scalar_tensor_tensor(
-            hid[1][:], by_column[:, HALF:O, :], -1.0, by_column[:, HALF:O, :], ALU.mult, ALU.max
-        )
+        hid_codes = [keep.tile([P, HALF], U32, name="hid_codes%d" % h, align_bytes=64) for h in range(2)]
+        hid_plane = [keep.tile([P, HALF], U8, name="hid_plane%d" % h, align_bytes=64) for h in range(2)]
+        by_column = [diff[h][:].rearrange("p t o -> p o t") for h in range(2)]
+        nc.scalar.activation(hid[0][:], by_column[0], ACT.Abs)
+        nc.vector.scalar_tensor_tensor(hid[1][:], by_column[1], -1.0, by_column[1], ALU.mult, ALU.max)
         for h in range(2):
-            cols = slice(HALF * h, HALF * (h + 1))
             nc.vector.quantize_mx(
-                out=hid_codes[:, cols].bitcast(E5M2X4),
-                scales=hid_plane[:, cols],
+                out=hid_codes[h][:].bitcast(E5M2X4),
+                scales=hid_plane[h][:],
                 in_=hid[h][:].rearrange("p o t -> p (o t)"),
             )
 
-        result = [keep.tile([P, O], F32, name="result%d" % n) for n in range(N // P)]
-        for n in range(N // P):
-            acc = psum.tile([P, O], F32, name="acc")
-            nc.tensor.matmul_mx(
-                out=acc[:],
-                lhsT=wb_codes[:, 2 * P * n : 2 * P * (n + 1)].bitcast(E2M1X4),
-                lhsT_scale=wb_plane[:, P * n : P * (n + 1)],
-                rhs=hid_codes[:].bitcast(E5M2X4),
-                rhs_scale=hid_plane[:],
-                start=True,
-                stop=True,
-            )
-            if n == 0:
-                nc.scalar.copy(out=result[n][:], in_=acc[:])
-                nc.scalar.dma_start(out=out[P * n : P * (n + 1), :], in_=result[n][:])
-            else:
-                nc.vector.tensor_copy(out=result[n][:], in_=acc[:])
-                nc.sync.dma_start(out=out[P * n : P * (n + 1), :], in_=result[n][:])
+        for h in range(2):
+            for n in range(N // P):
+                acc = psum.tile([P, HALF], F32, name="acc")
+                nc.tensor.matmul_mx(
+                    out=acc[:],
+                    lhsT=wb_codes[:, 2 * P * n : 2 * P * (n + 1)].bitcast(E2M1X4),
+                    lhsT_scale=wb_plane[:, P * n : P * (n + 1)],
+                    rhs=hid_codes[h][:].bitcast(E5M2X4),
+                    rhs_scale=hid_plane[h][:],
+                    start=True,
+                    stop=True,
+                )
+                result = keep.tile([P, HALF], F32, name="result%d%d" % (h, n))
+                place = out[P * n : P * (n + 1), HALF * h : HALF * (h + 1)]
+                if (h, n) == (1, 1):
+                    nc.vector.tensor_copy(out=result[:], in_=acc[:])
+                else:
+                    nc.scalar.copy(out=result[:], in_=acc[:])
+                if (h, n) == (1, 0):
+                    nc.scalar.dma_start(out=place, in_=result[:])
+                else:
+                    nc.sync.dma_start(out=place, in_=result[:])

@@ -33,6 +33,7 @@ def tile_list_tied_twoboards_one_plain_kernel(
     with ExitStack() as ctx:
         lists = ctx.enter_context(tc.tile_pool(name="lists", bufs=1))
         keep = ctx.enter_context(tc.tile_pool(name="keep", bufs=1))
+        reuse = ctx.enter_context(tc.tile_pool(name="reuse", bufs=1))
         psum = ctx.enter_context(tc.psum_pool(name="psum", bufs=8))
 
         l_tok_a = lists.tile([P, J // 16], U16, name="l_tok_a")
@@ -42,10 +43,10 @@ def tile_list_tied_twoboards_one_plain_kernel(
         l_get_a = lists.tile([P, O // 16], U16, name="l_get_a")
         l_get_b = lists.tile([P, O // 16], U16, name="l_get_b")
 
-        x_words = keep.tile([P, T], U16, name="x_words", tag="x_words", align_bytes=64)
-        x_plane = keep.tile([P, T], U8, name="x_plane", tag="x_plane", align_bytes=64)
+        x_words = keep.tile([P, T], U16, name="x_words", align_bytes=64)
+        x_plane = keep.tile([P, T], U8, name="x_plane", align_bytes=64)
         w_raw = keep.tile([P, R], U32, name="w_raw", align_bytes=64)
-        w_raw_plane = keep.tile([P, R], U8, name="w_raw_plane", align_bytes=64)
+        w_raw_plane = reuse.tile([P, R], U8, name="w_raw_plane", align_bytes=64, offset=0)
         w_codes = keep.tile([P, R], U32, name="w_codes", align_bytes=64)
         w_plane = keep.tile([P, R], U8, name="w_plane", align_bytes=64)
         wb_codes = keep.tile([P, 2 * N], U8, name="wb_codes", align_bytes=64)
@@ -53,50 +54,48 @@ def tile_list_tied_twoboards_one_plain_kernel(
 
         nc.vector.memset(x_plane[:].bitcast(I32), 0)
         nc.vector.memset(w_raw_plane[:].bitcast(I32), 0)
-        nc.vector.memset(wb_plane[:].bitcast(I32), 0)
 
         nc.sync.dma_start(l_tok_a[:], offs)
         nc.sync.dma_start(l_tok_b[:], offs2)
         nc.sync.dma_start(out=x_words[:].bitcast(I32), in_=xt_words[0].bitcast(I32))
-        nc.sync.dma_start(out=w_raw[:].bitcast(I32), in_=w_words[0].rearrange("p n t -> p (n t)").bitcast(I32))
+        nc.gpsimd.dma_start(out=w_raw[:].bitcast(I32), in_=w_words[0].rearrange("p n t -> p (n t)").bitcast(I32))
         for q in range(4):
             load_scale_rows(nc.scalar, x_plane, xt_scales, q)
-        for q in range(4):
+        for q in range(3):
             load_scale_rows(nc.sync, w_raw_plane, w_scales, q)
+        load_scale_rows(nc.gpsimd, w_raw_plane, w_scales, 3)
         nc.sync.dma_start(l_put_a[:], offs3)
         nc.sync.dma_start(l_put_b[:], offs4)
         nc.sync.dma_start(l_get_a[:], offs5)
         nc.sync.dma_start(l_get_b[:], offs6)
+        nc.gpsimd.memset(wb_plane[:].bitcast(I32), 0)
         nc.sync.dma_start(out=wb_codes[:].bitcast(I32), in_=wb_words[0].bitcast(I32))
         for q in range(4):
             load_scale_rows(nc.sync, wb_plane, wb_scales, q)
 
-        board_a = [keep.tile([P, C], F32, name="board_a%d" % t) for t in range(PACK - 1)]
-        board_b = [keep.tile([P, C], F32, name="board_b%d" % t) for t in range(PACK - 1)]
-        for t in range(PACK - 1):
-            nc.vector.memset(board_a[t][:], 0.0)
-            nc.vector.memset(board_b[t][:], 0.0)
+        board = {(s, t): keep.tile([P, C + 1], F32, name="board_%s%d" % (s, t)) for s in "ab" for t in range(PACK)}
+        by_need = [("a", 0), ("a", 1), ("b", 0), ("b", 1), ("a", 2), ("b", 2), ("a", 3), ("b", 3)]
+        for key in by_need[:5]:
+            nc.vector.memset(board[key][:], 0.0)
+        for key in by_need[5:]:
+            nc.gpsimd.memset(board[key][:], 0.0)
 
         nc.scalar.copy(
             out=w_codes[:].rearrange("p (t m) -> p m t", t=PACK), in_=w_raw[:].rearrange("p (m t) -> p m t", t=PACK)
         )
 
         xa_words = keep.tile([P, J], U16, name="xa_words", align_bytes=64)
-        xb_words = keep.tile([P, J], U16, name="xb_words", align_bytes=64)
+        xb_words = reuse.tile([P, J], U16, name="xb_words", align_bytes=64, offset=J)
         xa_plane = keep.tile([P, J], U8, name="xa_plane", align_bytes=64)
-        xb_plane = keep.tile([P, J], U8, name="xb_plane", align_bytes=64)
-        nc.vector.tensor_copy(xa_plane[:], x_plane[:].indirect(l_tok_a[:]))
-        nc.vector.tensor_copy(xb_plane[:], x_plane[:].indirect(l_tok_b[:]))
+        xb_plane = reuse.tile([P, J], U8, name="xb_plane", align_bytes=64, offset=0)
         nc.vector.tensor_copy(xa_words[:], x_words[:].indirect(l_tok_a[:]))
-        nc.vector.tensor_copy(xb_words[:], x_words[:].indirect(l_tok_b[:]))
+        nc.vector.tensor_copy(xa_plane[:], x_plane[:].indirect(l_tok_a[:]))
         nc.vector.tensor_copy(
             out=w_plane[:].rearrange("p (t m) -> p t m", t=PACK),
             in_=w_raw_plane[:].rearrange("p (m t) -> p t m", t=PACK),
         )
-        board_a.append(keep.tile([P, C], F32, name="board_a3", tag="x_plane", align_bytes=64))
-        board_b.append(keep.tile([P, C], F32, name="board_b3", tag="x_words", align_bytes=64))
-        nc.vector.memset(board_a[PACK - 1][:], 0.0)
-        nc.vector.memset(board_b[PACK - 1][:], 0.0)
+        nc.vector.tensor_copy(xb_plane[:], x_plane[:].indirect(l_tok_b[:]))
+        nc.vector.tensor_copy(xb_words[:], x_words[:].indirect(l_tok_b[:]))
 
         def first_product(t, words, plane):
             acc = psum.tile([P, J], F32, name="acc")
@@ -112,46 +111,68 @@ def tile_list_tied_twoboards_one_plain_kernel(
             )
             return acc
 
-        acc_a, acc_b = [], []
-        for t in range(PACK):
-            acc_a.append(first_product(t, xa_words, xa_plane))
-            acc_b.append(first_product(t, xb_words, xb_plane))
+        picked = {"a": (xa_words, xa_plane), "b": (xb_words, xb_plane)}
+        sums = {(s, t): first_product(t, *picked[s]) for s in "ab" for t in range(PACK)}
 
-        a_vals = [keep.tile([P, J], F32, name="a_vals%d" % t) for t in range(PACK)]
-        b_vals = [keep.tile([P, J], F32, name="b_vals%d" % t) for t in range(PACK)]
+        vals = {key: keep.tile([P, J], F32, name="vals_%s%d" % key) for key in by_need}
         a_read = [keep.tile([P, O], F32, name="a_read%d" % t) for t in range(PACK)]
         diff = [keep.tile([P, PACK, HALF], F32, name="diff%d" % h) for h in range(2)]
+        l_put = {"a": l_put_a, "b": l_put_b}
 
-        def leave_psum(t):
-            nc.scalar.copy(out=a_vals[t][:], in_=acc_a[t][:])
-            nc.vector.tensor_copy(out=b_vals[t][:], in_=acc_b[t][:])
+        def out_s(s, t):
+            nc.scalar.copy(out=vals[s, t][:], in_=sums[s, t][:])
 
-        def put(t):
-            nc.scalar.activation(board_a[t][:].indirect(l_put_a[:]), a_vals[t][:], ACT.Copy)
-            nc.vector.tensor_copy(board_b[t][:].indirect(l_put_b[:]), b_vals[t][:])
+        def out_v(s, t):
+            nc.vector.tensor_copy(out=vals[s, t][:], in_=sums[s, t][:])
 
-        def get(t):
-            nc.scalar.activation(a_read[t][:], board_a[t][:].indirect(l_get_a[:]), ACT.Copy)
+        def put_s(s, t):
+            nc.scalar.activation(board[s, t][:].indirect(l_put[s][:]), vals[s, t][:], ACT.Copy)
+
+        def put_v(s, t):
+            nc.vector.tensor_copy(board[s, t][:].indirect(l_put[s][:]), vals[s, t][:])
+
+        def get_a(t):
+            nc.scalar.activation(a_read[t][:], board["a", t][:].indirect(l_get_a[:]), ACT.Copy)
+
+        def get_b(t):
             for h in range(2):
                 picks = l_get_b[:, HALF // 16 * h : HALF // 16 * (h + 1)]
                 nc.vector.tensor_tensor(
-                    diff[h][:, t, :], board_b[t][:].indirect(picks), a_read[t][:, HALF * h : HALF * (h + 1)], ALU.subtract
+                    diff[h][:, t, :], board["b", t][:].indirect(picks), a_read[t][:, HALF * h : HALF * (h + 1)], ALU.subtract
                 )
 
-        leave_psum(0)
-        for t in range(PACK):
-            put(t)
-            if t + 1 < PACK:
-                leave_psum(t + 1)
-            get(t)
+        out_s("a", 0)
+        out_s("a", 1)
+        put_s("a", 0)
+        put_v("a", 1)
+        out_s("b", 1)
+        out_v("b", 0)
+        out_v("b", 2)
+        get_a(0)
+        put_v("b", 0)
+        put_s("b", 1)
+        out_v("b", 3)
+        out_s("a", 2)
+        out_s("a", 3)
+        put_v("b", 2)
+        put_s("a", 2)
+        get_b(0)
+        get_a(1)
+        put_v("b", 3)
+        put_s("a", 3)
+        get_b(1)
+        get_a(2)
+        get_b(2)
+        get_a(3)
+        get_b(3)
 
         hid = [keep.tile([P, HALF, PACK], BF16, name="hid%d" % h, align_bytes=64) for h in range(2)]
         hid_codes = [keep.tile([P, HALF], U32, name="hid_codes%d" % h, align_bytes=64) for h in range(2)]
         hid_plane = [keep.tile([P, HALF], U8, name="hid_plane%d" % h, align_bytes=64) for h in range(2)]
-        by_column = [diff[h][:].rearrange("p t o -> p o t") for h in range(2)]
-        nc.scalar.activation(hid[0][:], by_column[0], ACT.Abs)
-        nc.vector.scalar_tensor_tensor(hid[1][:], by_column[1], -1.0, by_column[1], ALU.mult, ALU.max)
         for h in range(2):
+            nc.scalar.activation(
+                hid[h][:].rearrange("p (c i) t -> p c t i", i=4), diff[h][:].rearrange("p t (c i) -> p c t i", i=4), ACT.Abs
+            )
             nc.vector.quantize_mx(
                 out=hid_codes[h][:].bitcast(E5M2X4),
                 scales=hid_plane[h][:],
@@ -172,7 +193,7 @@ def tile_list_tied_twoboards_one_plain_kernel(
                 )
                 result = keep.tile([P, HALF], F32, name="result%d%d" % (h, n))
                 place = out[P * n : P * (n + 1), HALF * h : HALF * (h + 1)]
-                if (h, n) == (1, 1):
+                if (h, n) != (1, 0):
                     nc.vector.tensor_copy(out=result[:], in_=acc[:])
                 else:
                     nc.scalar.copy(out=result[:], in_=acc[:])

@@ -19,11 +19,22 @@ ALU = mybir.AluOpType
 
 P = 128
 PACK = 4
+QUADRANTS = 4
+PER_COLUMN = 16
+BANKS = 8
 HALF = O // 2
+QUARTER = O // 4
+RUN = 4
+BOARD_WIDTH = C + 1
+VECTOR_CLEARS = 5
 
 
 def load_scale_rows(queue, plane, scales, q):
     queue.dma_start(out=plane[32 * q : 32 * q + 4, :].bitcast(I32), in_=scales[0, 4 * q : 4 * q + 4, :].bitcast(I32))
+
+
+def list_columns(entries):
+    return slice(entries.start // PER_COLUMN, entries.stop // PER_COLUMN)
 
 
 def tile_list_tied_twoboards_one_plain_kernel(
@@ -34,76 +45,77 @@ def tile_list_tied_twoboards_one_plain_kernel(
         lists = ctx.enter_context(tc.tile_pool(name="lists", bufs=1))
         keep = ctx.enter_context(tc.tile_pool(name="keep", bufs=1))
         reuse = ctx.enter_context(tc.tile_pool(name="reuse", bufs=1))
-        psum = ctx.enter_context(tc.psum_pool(name="psum", bufs=8))
+        psum = ctx.enter_context(tc.psum_pool(name="psum", bufs=BANKS))
 
-        l_tok_a = lists.tile([P, J // 16], U16, name="l_tok_a")
-        l_tok_b = lists.tile([P, J // 16], U16, name="l_tok_b")
-        l_put_a = lists.tile([P, J // 16], U16, name="l_put_a")
-        l_put_b = lists.tile([P, J // 16], U16, name="l_put_b")
-        l_get_a = lists.tile([P, O // 16], U16, name="l_get_a")
-        l_get_b = lists.tile([P, O // 16], U16, name="l_get_b")
+        tokens = {s: lists.tile([P, J // PER_COLUMN], U16, name="tokens_" + s) for s in "ab"}
+        places = {s: lists.tile([P, J // PER_COLUMN], U16, name="places_" + s) for s in "ab"}
+        reads = {s: lists.tile([P, O // PER_COLUMN], U16, name="reads_" + s) for s in "ab"}
 
         x_words = keep.tile([P, T], U16, name="x_words", align_bytes=64)
         x_plane = keep.tile([P, T], U8, name="x_plane", align_bytes=64)
-        w_raw = keep.tile([P, R], U32, name="w_raw", align_bytes=64)
+        w_raw_words = keep.tile([P, R], U32, name="w_raw_words", align_bytes=64)
         w_raw_plane = reuse.tile([P, R], U8, name="w_raw_plane", align_bytes=64, offset=0)
-        w_codes = keep.tile([P, R], U32, name="w_codes", align_bytes=64)
-        w_plane = keep.tile([P, R], U8, name="w_plane", align_bytes=64)
-        wb_codes = keep.tile([P, 2 * N], U8, name="wb_codes", align_bytes=64)
+        w_dealt_words = keep.tile([P, R], U32, name="w_dealt_words", align_bytes=64)
+        w_dealt_plane = keep.tile([P, R], U8, name="w_dealt_plane", align_bytes=64)
+        wb_packed = keep.tile([P, 2 * N], U8, name="wb_packed", align_bytes=64)
         wb_plane = keep.tile([P, N], U8, name="wb_plane", align_bytes=64)
 
         nc.vector.memset(x_plane[:].bitcast(I32), 0)
         nc.vector.memset(w_raw_plane[:].bitcast(I32), 0)
 
-        nc.sync.dma_start(l_tok_a[:], offs)
-        nc.sync.dma_start(l_tok_b[:], offs2)
+        nc.sync.dma_start(tokens["a"][:], offs)
+        nc.sync.dma_start(tokens["b"][:], offs2)
         nc.sync.dma_start(out=x_words[:].bitcast(I32), in_=xt_words[0].bitcast(I32))
-        nc.gpsimd.dma_start(out=w_raw[:].bitcast(I32), in_=w_words[0].rearrange("p n t -> p (n t)").bitcast(I32))
-        for q in range(4):
+        nc.gpsimd.dma_start(out=w_raw_words[:].bitcast(I32), in_=w_words[0].rearrange("p n t -> p (n t)").bitcast(I32))
+        for q in range(QUADRANTS):
             load_scale_rows(nc.scalar, x_plane, xt_scales, q)
-        for q in range(3):
+        for q in range(QUADRANTS - 1):
             load_scale_rows(nc.sync, w_raw_plane, w_scales, q)
-        load_scale_rows(nc.gpsimd, w_raw_plane, w_scales, 3)
-        nc.sync.dma_start(l_put_a[:], offs3)
-        nc.sync.dma_start(l_put_b[:], offs4)
-        nc.sync.dma_start(l_get_a[:], offs5)
-        nc.sync.dma_start(l_get_b[:], offs6)
+        load_scale_rows(nc.gpsimd, w_raw_plane, w_scales, QUADRANTS - 1)
+        nc.sync.dma_start(places["a"][:], offs3)
+        nc.sync.dma_start(places["b"][:], offs4)
+        nc.sync.dma_start(reads["a"][:], offs5)
+        nc.sync.dma_start(reads["b"][:], offs6)
         nc.gpsimd.memset(wb_plane[:].bitcast(I32), 0)
-        nc.sync.dma_start(out=wb_codes[:].bitcast(I32), in_=wb_words[0].bitcast(I32))
-        for q in range(4):
+        nc.sync.dma_start(out=wb_packed[:].bitcast(I32), in_=wb_words[0].bitcast(I32))
+        for q in range(QUADRANTS):
             load_scale_rows(nc.sync, wb_plane, wb_scales, q)
 
-        board = {(s, t): keep.tile([P, C + 1], F32, name="board_%s%d" % (s, t)) for s in "ab" for t in range(PACK)}
-        by_need = [("a", 0), ("a", 1), ("b", 0), ("b", 1), ("a", 2), ("b", 2), ("a", 3), ("b", 3)]
-        for key in by_need[:5]:
+        board = {
+            (s, t): keep.tile([P, BOARD_WIDTH], F32, name="board_%s%d" % (s, t)) for s in "ab" for t in range(PACK)
+        }
+        scatter_order = [("a", 0), ("a", 1), ("b", 0), ("b", 1), ("a", 2), ("b", 2), ("a", 3), ("b", 3)]
+        for key in scatter_order[:VECTOR_CLEARS]:
             nc.vector.memset(board[key][:], 0.0)
-        for key in by_need[5:]:
+        for key in scatter_order[VECTOR_CLEARS:]:
             nc.gpsimd.memset(board[key][:], 0.0)
 
-        nc.scalar.copy(
-            out=w_codes[:].rearrange("p (t m) -> p m t", t=PACK), in_=w_raw[:].rearrange("p (m t) -> p m t", t=PACK)
-        )
+        for t in range(0, PACK, 2):
+            nc.scalar.copy(
+                out=w_dealt_words[:, P * t : P * (t + 2)].rearrange("p (t m) -> p m t", t=2),
+                in_=w_raw_words[:].rearrange("p (m t) -> p m t", t=PACK)[:, :, t : t + 2],
+            )
 
         xa_words = keep.tile([P, J], U16, name="xa_words", align_bytes=64)
         xb_words = reuse.tile([P, J], U16, name="xb_words", align_bytes=64, offset=J)
         xa_plane = keep.tile([P, J], U8, name="xa_plane", align_bytes=64)
         xb_plane = reuse.tile([P, J], U8, name="xb_plane", align_bytes=64, offset=0)
-        nc.vector.tensor_copy(xa_words[:], x_words[:].indirect(l_tok_a[:]))
-        nc.vector.tensor_copy(xa_plane[:], x_plane[:].indirect(l_tok_a[:]))
+        nc.vector.tensor_copy(xa_words[:], x_words[:].indirect(tokens["a"][:]))
+        nc.vector.tensor_copy(xa_plane[:], x_plane[:].indirect(tokens["a"][:]))
         nc.vector.tensor_copy(
-            out=w_plane[:].rearrange("p (t m) -> p t m", t=PACK),
+            out=w_dealt_plane[:].rearrange("p (t m) -> p t m", t=PACK),
             in_=w_raw_plane[:].rearrange("p (m t) -> p t m", t=PACK),
         )
-        nc.vector.tensor_copy(xb_plane[:], x_plane[:].indirect(l_tok_b[:]))
-        nc.vector.tensor_copy(xb_words[:], x_words[:].indirect(l_tok_b[:]))
+        nc.vector.tensor_copy(xb_plane[:], x_plane[:].indirect(tokens["b"][:]))
+        nc.vector.tensor_copy(xb_words[:], x_words[:].indirect(tokens["b"][:]))
 
         def first_product(t, words, plane):
             acc = psum.tile([P, J], F32, name="acc")
             cols = slice(P * t, P * (t + 1))
             nc.tensor.matmul_mx(
                 out=acc[:],
-                lhsT=w_codes[:, cols].bitcast(E4M3X4),
-                lhsT_scale=w_plane[:, cols],
+                lhsT=w_dealt_words[:, cols].bitcast(E4M3X4),
+                lhsT_scale=w_dealt_plane[:, cols],
                 rhs=words[:].bitcast(E2M1X4),
                 rhs_scale=plane[:],
                 start=True,
@@ -114,67 +126,73 @@ def tile_list_tied_twoboards_one_plain_kernel(
         picked = {"a": (xa_words, xa_plane), "b": (xb_words, xb_plane)}
         sums = {(s, t): first_product(t, *picked[s]) for s in "ab" for t in range(PACK)}
 
-        vals = {key: keep.tile([P, J], F32, name="vals_%s%d" % key) for key in by_need}
+        staged = {key: keep.tile([P, J], F32, name="staged_%s%d" % key) for key in scatter_order}
         a_read = [keep.tile([P, O], F32, name="a_read%d" % t) for t in range(PACK)]
-        diff = [keep.tile([P, PACK, HALF], F32, name="diff%d" % h) for h in range(2)]
-        l_put = {"a": l_put_a, "b": l_put_b}
+        diff = keep.tile([P, PACK, O], F32, name="diff")
 
-        def out_s(s, t):
-            nc.scalar.copy(out=vals[s, t][:], in_=sums[s, t][:])
+        def stage_on_scalar(s, t):
+            nc.scalar.copy(out=staged[s, t][:], in_=sums[s, t][:])
 
-        def out_v(s, t):
-            nc.vector.tensor_copy(out=vals[s, t][:], in_=sums[s, t][:])
+        def stage_on_vector(s, t):
+            nc.vector.tensor_copy(out=staged[s, t][:], in_=sums[s, t][:])
 
-        def put_s(s, t):
-            nc.scalar.activation(board[s, t][:].indirect(l_put[s][:]), vals[s, t][:], ACT.Copy)
+        def scatter_on_scalar(s, t):
+            nc.scalar.activation(board[s, t][:].indirect(places[s][:]), staged[s, t][:], ACT.Copy)
 
-        def put_v(s, t):
-            nc.vector.tensor_copy(board[s, t][:].indirect(l_put[s][:]), vals[s, t][:])
+        def scatter_on_vector(s, t):
+            nc.vector.tensor_copy(board[s, t][:].indirect(places[s][:]), staged[s, t][:])
 
-        def get_a(t):
-            nc.scalar.activation(a_read[t][:], board["a", t][:].indirect(l_get_a[:]), ACT.Copy)
+        def read_a(t, entries):
+            window = board["a", t][:].indirect(reads["a"][:, list_columns(entries)])
+            nc.scalar.activation(a_read[t][:, entries], window, ACT.Copy)
 
-        def get_b(t):
-            for h in range(2):
-                picks = l_get_b[:, HALF // 16 * h : HALF // 16 * (h + 1)]
-                nc.vector.tensor_tensor(
-                    diff[h][:, t, :], board["b", t][:].indirect(picks), a_read[t][:, HALF * h : HALF * (h + 1)], ALU.subtract
-                )
+        def read_b_minus_a(t, entries):
+            window = board["b", t][:].indirect(reads["b"][:, list_columns(entries)])
+            nc.vector.tensor_tensor(diff[:, t, entries], window, a_read[t][:, entries], ALU.subtract)
 
-        out_s("a", 0)
-        out_s("a", 1)
-        put_s("a", 0)
-        put_v("a", 1)
-        out_s("b", 1)
-        out_v("b", 0)
-        out_v("b", 2)
-        get_a(0)
-        put_v("b", 0)
-        put_s("b", 1)
-        out_v("b", 3)
-        out_s("a", 2)
-        out_s("a", 3)
-        put_v("b", 2)
-        put_s("a", 2)
-        get_b(0)
-        get_a(1)
-        put_v("b", 3)
-        put_s("a", 3)
-        get_b(1)
-        get_a(2)
-        get_b(2)
-        get_a(3)
-        get_b(3)
+        everything = slice(0, O)
+        halves = [slice(HALF * h, HALF * (h + 1)) for h in range(2)]
+        stage_on_scalar("a", 0)
+        stage_on_scalar("a", 1)
+        scatter_on_scalar("a", 0)
+        scatter_on_vector("a", 1)
+        stage_on_scalar("b", 1)
+        stage_on_vector("b", 0)
+        stage_on_vector("a", 2)
+        stage_on_vector("b", 2)
+        read_a(0, everything)
+        scatter_on_vector("b", 0)
+        scatter_on_scalar("b", 1)
+        stage_on_vector("b", 3)
+        stage_on_vector("a", 3)
+        read_a(1, everything)
+        scatter_on_vector("b", 2)
+        scatter_on_scalar("a", 2)
+        read_b_minus_a(0, everything)
+        read_a(2, everything)
+        scatter_on_vector("b", 3)
+        scatter_on_scalar("a", 3)
+        read_b_minus_a(1, everything)
+        read_b_minus_a(2, everything)
+        for entries in halves:
+            read_a(PACK - 1, entries)
+        for entries in halves:
+            read_b_minus_a(PACK - 1, entries)
 
         hid = [keep.tile([P, HALF, PACK], BF16, name="hid%d" % h, align_bytes=64) for h in range(2)]
-        hid_codes = [keep.tile([P, HALF], U32, name="hid_codes%d" % h, align_bytes=64) for h in range(2)]
+        hid_words = [keep.tile([P, HALF], U32, name="hid_words%d" % h, align_bytes=64) for h in range(2)]
         hid_plane = [keep.tile([P, HALF], U8, name="hid_plane%d" % h, align_bytes=64) for h in range(2)]
-        for h in range(2):
+        for h, width in ((0, HALF), (1, HALF - QUARTER)):
             nc.scalar.activation(
-                hid[h][:].rearrange("p (c i) t -> p c t i", i=4), diff[h][:].rearrange("p t (c i) -> p c t i", i=4), ACT.Abs
+                hid[h][:, :width, :].rearrange("p (c i) t -> p c t i", i=RUN),
+                diff[:, :, HALF * h : HALF * h + width].rearrange("p t (c i) -> p c t i", i=RUN),
+                ACT.Abs,
             )
+        last = diff[:].rearrange("p t o -> p o t")[:, O - QUARTER :, :]
+        nc.vector.scalar_tensor_tensor(hid[1][:, HALF - QUARTER :, :], last, -1.0, last, ALU.mult, ALU.max)
+        for h in range(2):
             nc.vector.quantize_mx(
-                out=hid_codes[h][:].bitcast(E5M2X4),
+                out=hid_words[h][:].bitcast(E5M2X4),
                 scales=hid_plane[h][:],
                 in_=hid[h][:].rearrange("p o t -> p (o t)"),
             )
@@ -184,20 +202,17 @@ def tile_list_tied_twoboards_one_plain_kernel(
                 acc = psum.tile([P, HALF], F32, name="acc")
                 nc.tensor.matmul_mx(
                     out=acc[:],
-                    lhsT=wb_codes[:, 2 * P * n : 2 * P * (n + 1)].bitcast(E2M1X4),
+                    lhsT=wb_packed[:, 2 * P * n : 2 * P * (n + 1)].bitcast(E2M1X4),
                     lhsT_scale=wb_plane[:, P * n : P * (n + 1)],
-                    rhs=hid_codes[h][:].bitcast(E5M2X4),
+                    rhs=hid_words[h][:].bitcast(E5M2X4),
                     rhs_scale=hid_plane[h][:],
                     start=True,
                     stop=True,
                 )
                 result = keep.tile([P, HALF], F32, name="result%d%d" % (h, n))
-                place = out[P * n : P * (n + 1), HALF * h : HALF * (h + 1)]
-                if (h, n) != (1, 0):
+                if (h, n) == (1, 1):
                     nc.vector.tensor_copy(out=result[:], in_=acc[:])
                 else:
                     nc.scalar.copy(out=result[:], in_=acc[:])
-                if (h, n) == (1, 0):
-                    nc.scalar.dma_start(out=place, in_=result[:])
-                else:
-                    nc.sync.dma_start(out=place, in_=result[:])
+                queue = nc.scalar if (h, n) == (1, 0) else nc.sync
+                queue.dma_start(out=out[P * n : P * (n + 1), halves[h]], in_=result[:])

@@ -60,8 +60,8 @@ def tile_list_tied_twoboards_one_plain_kernel(
         wb_packed = keep.tile([P, 2 * N], U8, name="wb_packed", align_bytes=64)
         wb_plane = keep.tile([P, N], U8, name="wb_plane", align_bytes=64)
 
-        nc.vector.memset(x_plane[:].bitcast(I32), 0)
         nc.vector.memset(w_raw_plane[:].bitcast(I32), 0)
+        nc.vector.memset(x_plane[:].bitcast(I32), 0)
 
         nc.sync.dma_start(tokens["a"][:], offs)
         nc.sync.dma_start(tokens["b"][:], offs2)
@@ -102,10 +102,8 @@ def tile_list_tied_twoboards_one_plain_kernel(
         xb_plane = reuse.tile([P, J], U8, name="xb_plane", align_bytes=64, offset=0)
         nc.vector.tensor_copy(xa_words[:], x_words[:].indirect(tokens["a"][:]))
         nc.vector.tensor_copy(xa_plane[:], x_plane[:].indirect(tokens["a"][:]))
-        nc.vector.tensor_copy(
-            out=w_dealt_plane[:].rearrange("p (t m) -> p t m", t=PACK),
-            in_=w_raw_plane[:].rearrange("p (m t) -> p t m", t=PACK),
-        )
+        for t in range(PACK):
+            nc.vector.tensor_copy(out=w_dealt_plane[:, P * t : P * (t + 1)], in_=w_raw_plane[:, t::PACK])
         nc.vector.tensor_copy(xb_plane[:], x_plane[:].indirect(tokens["b"][:]))
         nc.vector.tensor_copy(xb_words[:], x_words[:].indirect(tokens["b"][:]))
 

from contextlib import ExitStack

import concourse.mybir as mybir

K, T, J, R, C, O, N = 512, 2048, 256, 512, 512, 256, 256
FLOPS = 2 * K * R * 2 * J + 2 * R * N * O

F32 = mybir.dt.float32
BF16 = mybir.dt.bfloat16
I32 = mybir.dt.int32
U32 = mybir.dt.uint32
U16 = mybir.dt.uint16
U8 = mybir.dt.uint8
E4M3X4 = mybir.dt.float8_e4m3fn_x4
E5M2X4 = mybir.dt.float8_e5m2_x4
E2M1X4 = mybir.dt.float4_e2m1fn_x4
ACT = mybir.ActivationFunctionType
ALU = mybir.AluOpType

P = 128
PACK = 4
QUADRANTS = 4
PER_COLUMN = 16
BANKS = 8
HALF = O // 2
QUARTER = O // 4
RUN = 4
BOARD_WIDTH = C + 1
VECTOR_CLEARS = 5


def load_scale_rows(queue, plane, scales, q):
    queue.dma_start(out=plane[32 * q : 32 * q + 4, :].bitcast(I32), in_=scales[0, 4 * q : 4 * q + 4, :].bitcast(I32))


def list_columns(entries):
    return slice(entries.start // PER_COLUMN, entries.stop // PER_COLUMN)


def tile_list_tied_twoboards_one_plain_kernel(
    tc, xt_words, xt_scales, w_words, w_scales, wb_words, wb_scales, offs, offs2, offs3, offs4, offs5, offs6, out
):
    nc = tc.nc
    with ExitStack() as ctx:
        lists = ctx.enter_context(tc.tile_pool(name="lists", bufs=1))
        keep = ctx.enter_context(tc.tile_pool(name="keep", bufs=1))
        reuse = ctx.enter_context(tc.tile_pool(name="reuse", bufs=1))
        psum = ctx.enter_context(tc.psum_pool(name="psum", bufs=BANKS))

        tokens = {s: lists.tile([P, J // PER_COLUMN], U16, name="tokens_" + s) for s in "ab"}
        places = {s: lists.tile([P, J // PER_COLUMN], U16, name="places_" + s) for s in "ab"}
        reads = {s: lists.tile([P, O // PER_COLUMN], U16, name="reads_" + s) for s in "ab"}

        x_words = keep.tile([P, T], U16, name="x_words", align_bytes=64)
        x_plane = keep.tile([P, T], U8, name="x_plane", align_bytes=64)
        w_raw_words = keep.tile([P, R], U32, name="w_raw_words", align_bytes=64)
        w_raw_plane = reuse.tile([P, R], U8, name="w_raw_plane", align_bytes=64, offset=0)
        w_dealt_words = keep.tile([P, R], U32, name="w_dealt_words", align_bytes=64)
        w_dealt_plane = keep.tile([P, R], U8, name="w_dealt_plane", align_bytes=64)
        wb_packed = keep.tile([P, 2 * N], U8, name="wb_packed", align_bytes=64)
        wb_plane = keep.tile([P, N], U8, name="wb_plane", align_bytes=64)

        nc.vector.memset(w_raw_plane[:].bitcast(I32), 0)
        nc.vector.memset(x_plane[:].bitcast(I32), 0)

        nc.sync.dma_start(tokens["a"][:], offs)
        nc.sync.dma_start(tokens["b"][:], offs2)
        nc.sync.dma_start(out=x_words[:].bitcast(I32), in_=xt_words[0].bitcast(I32))
        nc.gpsimd.dma_start(out=w_raw_words[:].bitcast(I32), in_=w_words[0].rearrange("p n t -> p (n t)").bitcast(I32))
        for q in range(QUADRANTS):
            load_scale_rows(nc.scalar, x_plane, xt_scales, q)
        for q in range(QUADRANTS - 1):
            load_scale_rows(nc.sync, w_raw_plane, w_scales, q)
        load_scale_rows(nc.gpsimd, w_raw_plane, w_scales, QUADRANTS - 1)
        nc.sync.dma_start(places["a"][:], offs3)
        nc.sync.dma_start(places["b"][:], offs4)
        nc.sync.dma_start(reads["a"][:], offs5)
        nc.sync.dma_start(reads["b"][:], offs6)
        nc.gpsimd.memset(wb_plane[:].bitcast(I32), 0)
        nc.sync.dma_start(out=wb_packed[:].bitcast(I32), in_=wb_words[0].bitcast(I32))
        for q in range(QUADRANTS):
            load_scale_rows(nc.sync, wb_plane, wb_scales, q)

        board = {
            (s, t): keep.tile([P, BOARD_WIDTH], F32, name="board_%s%d" % (s, t)) for s in "ab" for t in range(PACK)
        }
        scatter_order = [("a", 0), ("a", 1), ("b", 0), ("b", 1), ("a", 2), ("b", 2), ("a", 3), ("b", 3)]
        for key in scatter_order[:VECTOR_CLEARS]:
            nc.vector.memset(board[key][:], 0.0)
        for key in scatter_order[VECTOR_CLEARS:]:
            nc.gpsimd.memset(board[key][:], 0.0)

        for t in range(0, PACK, 2):
            nc.scalar.copy(
                out=w_dealt_words[:, P * t : P * (t + 2)].rearrange("p (t m) -> p m t", t=2),
                in_=w_raw_words[:].rearrange("p (m t) -> p m t", t=PACK)[:, :, t : t + 2],
            )

        xa_words = keep.tile([P, J], U16, name="xa_words", align_bytes=64)
        xb_words = reuse.tile([P, J], U16, name="xb_words", align_bytes=64, offset=J)
        xa_plane = keep.tile([P, J], U8, name="xa_plane", align_bytes=64)
        xb_plane = reuse.tile([P, J], U8, name="xb_plane", align_bytes=64, offset=0)
        nc.vector.tensor_copy(xa_words[:], x_words[:].indirect(tokens["a"][:]))
        nc.vector.tensor_copy(xa_plane[:], x_plane[:].indirect(tokens["a"][:]))
        for t in range(PACK):
            nc.vector.tensor_copy(out=w_dealt_plane[:, P * t : P * (t + 1)], in_=w_raw_plane[:, t::PACK])
        nc.vector.tensor_copy(xb_plane[:], x_plane[:].indirect(tokens["b"][:]))
        nc.vector.tensor_copy(xb_words[:], x_words[:].indirect(tokens["b"][:]))

        def first_product(t, words, plane):
            acc = psum.tile([P, J], F32, name="acc")
            cols = slice(P * t, P * (t + 1))
            nc.tensor.matmul_mx(
                out=acc[:],
                lhsT=w_dealt_words[:, cols].bitcast(E4M3X4),
                lhsT_scale=w_dealt_plane[:, cols],
                rhs=words[:].bitcast(E2M1X4),
                rhs_scale=plane[:],
                start=True,
                stop=True,
            )
            return acc

        picked = {"a": (xa_words, xa_plane), "b": (xb_words, xb_plane)}
        sums = {(s, t): first_product(t, *picked[s]) for s in "ab" for t in range(PACK)}

        staged = {key: keep.tile([P, J], F32, name="staged_%s%d" % key) for key in scatter_order}
        a_read = [keep.tile([P, O], F32, name="a_read%d" % t) for t in range(PACK)]
        diff = keep.tile([P, PACK, O], F32, name="diff")

        def stage_on_scalar(s, t):
            nc.scalar.copy(out=staged[s, t][:], in_=sums[s, t][:])

        def stage_on_vector(s, t):
            nc.vector.tensor_copy(out=staged[s, t][:], in_=sums[s, t][:])

        def scatter_on_scalar(s, t):
            nc.scalar.activation(board[s, t][:].indirect(places[s][:]), staged[s, t][:], ACT.Copy)

        def scatter_on_vector(s, t):
            nc.vector.tensor_copy(board[s, t][:].indirect(places[s][:]), staged[s, t][:])

        def read_a(t, entries):
            window = board["a", t][:].indirect(reads["a"][:, list_columns(entries)])
            nc.scalar.activation(a_read[t][:, entries], window, ACT.Copy)

        def read_b_minus_a(t, entries):
            window = board["b", t][:].indirect(reads["b"][:, list_columns(entries)])
            nc.vector.tensor_tensor(diff[:, t, entries], window, a_read[t][:, entries], ALU.subtract)

        everything = slice(0, O)
        halves = [slice(HALF * h, HALF * (h + 1)) for h in range(2)]
        stage_on_scalar("a", 0)
        stage_on_scalar("a", 1)
        scatter_on_scalar("a", 0)
        scatter_on_vector("a", 1)
        stage_on_scalar("b", 1)
        stage_on_vector("b", 0)
        stage_on_vector("a", 2)
        stage_on_vector("b", 2)
        read_a(0, everything)
        scatter_on_vector("b", 0)
        scatter_on_scalar("b", 1)
        stage_on_vector("b", 3)
        stage_on_vector("a", 3)
        read_a(1, everything)
        scatter_on_vector("b", 2)
        scatter_on_scalar("a", 2)
        read_b_minus_a(0, everything)
        read_a(2, everything)
        scatter_on_vector("b", 3)
        scatter_on_scalar("a", 3)
        read_b_minus_a(1, everything)
        read_b_minus_a(2, everything)
        for entries in halves:
            read_a(PACK - 1, entries)
        for entries in halves:
            read_b_minus_a(PACK - 1, entries)

        hid = [keep.tile([P, HALF, PACK], BF16, name="hid%d" % h, align_bytes=64) for h in range(2)]
        hid_words = [keep.tile([P, HALF], U32, name="hid_words%d" % h, align_bytes=64) for h in range(2)]
        hid_plane = [keep.tile([P, HALF], U8, name="hid_plane%d" % h, align_bytes=64) for h in range(2)]
        for h, width in ((0, HALF), (1, HALF - QUARTER)):
            nc.scalar.activation(
                hid[h][:, :width, :].rearrange("p (c i) t -> p c t i", i=RUN),
                diff[:, :, HALF * h : HALF * h + width].rearrange("p t (c i) -> p c t i", i=RUN),
                ACT.Abs,
            )
        last = diff[:].rearrange("p t o -> p o t")[:, O - QUARTER :, :]
        nc.vector.scalar_tensor_tensor(hid[1][:, HALF - QUARTER :, :], last, -1.0, last, ALU.mult, ALU.max)
        for h in range(2):
            nc.vector.quantize_mx(
                out=hid_words[h][:].bitcast(E5M2X4),
                scales=hid_plane[h][:],
                in_=hid[h][:].rearrange("p o t -> p (o t)"),
            )

        for h in range(2):
            for n in range(N // P):
                acc = psum.tile([P, HALF], F32, name="acc")
                nc.tensor.matmul_mx(
                    out=acc[:],
                    lhsT=wb_packed[:, 2 * P * n : 2 * P * (n + 1)].bitcast(E2M1X4),
                    lhsT_scale=wb_plane[:, P * n : P * (n + 1)],
                    rhs=hid_words[h][:].bitcast(E5M2X4),
                    rhs_scale=hid_plane[h][:],
                    start=True,
                    stop=True,
                )
                result = keep.tile([P, HALF], F32, name="result%d%d" % (h, n))
                if (h, n) == (1, 1):
                    nc.vector.tensor_copy(out=result[:], in_=acc[:])
                else:
                    nc.scalar.copy(out=result[:], in_=acc[:])
                queue = nc.scalar if (h, n) == (1, 0) else nc.sync
                queue.dma_start(out=out[P * n : P * (n + 1), halves[h]], in_=result[:])
